import numpy as np
import ml_dtypes


def mxq(x, axis, fmt="e4m3"):
    dtype, down = {"e4m3": (ml_dtypes.float8_e4m3fn, 7), "e5m2": (ml_dtypes.float8_e5m2, 14)}[fmt]
    v = np.moveaxis(np.asarray(x, np.float32).astype(ml_dtypes.bfloat16).astype(np.float64), axis, -1)
    blocks = v.reshape(v.shape[:-1] + (-1, 32))
    amax = np.abs(blocks).max(-1, keepdims=True)
    byte = np.maximum(np.where(amax > 0, np.frexp(amax)[1] - 1 + 127, 0) - down, 1)
    scale = np.exp2(byte - 127.0)
    codes = (blocks / scale).astype(np.float32).astype(dtype).astype(np.float64)
    return np.moveaxis((codes * scale).reshape(v.shape), -1, axis)


WIDE = False


def mx_kscale(k):
    if not WIDE:
        return np.ones(k)
    levels = np.array([10, -10, 5, -5, 0])
    if k % 512:
        return np.exp2(np.random.permutation(np.resize(levels, k // 32))).repeat(32)
    a = np.empty((k // 512, 16))
    for p in range(k // 512):
        a[p, :8] = np.random.permutation(np.resize(levels, 8))
        for g in range(8):
            far = levels[np.abs(levels - a[p, g]) >= 10]
            a[p, g + 8] = far[np.random.randint(len(far))]
    return np.exp2(a.ravel()).repeat(32)


BF16 = ml_dtypes.bfloat16


def bf(x):
    return np.asarray(x, np.float32).astype(BF16)


def f64(x):
    return np.asarray(x).astype(np.float64)


E2M1 = np.array([0.0, 0.5, 1.0, 1.5, 2.0, 3.0, 4.0, 6.0, -0.0, -0.5, -1.0, -1.5, -2.0, -3.0, -4.0, -6.0])


def pack_weight(w, fmt):
    k, n = w.shape
    w = f64(bf(w)).reshape(k // 32, 32, n)
    amax = np.abs(w).max(1)
    if fmt == "e4m3":
        byte = np.frexp(amax)[1] - 1 + 127 - 7
    else:
        mant, ex = np.frexp(amax / 6.0)
        byte = np.where(mant > 0.5, ex, ex - 1) + 127
    byte = np.clip(np.where(amax > 0, byte, 1), 1, 254)
    scaled = (w * np.exp2(127.0 - byte)[:, None, :]).reshape(k, n).astype(np.float32)
    by_word = np.ascontiguousarray(scaled.reshape(k // 512, 128, 4, n).transpose(0, 1, 3, 2))
    if fmt == "e4m3":
        words = by_word.astype(ml_dtypes.float8_e4m3fn).view(np.uint8)
    else:
        c = by_word.astype(ml_dtypes.float4_e2m1fn).view(np.uint8) & 0xF
        words = c[..., 0::2] | (c[..., 1::2] << 4)
    return np.ascontiguousarray(words), np.ascontiguousarray(byte.astype(np.uint8).reshape(k // 512, 16, n))


def unpack_weight(words, scales, fmt):
    g, p, n, _ = words.shape
    if fmt == "e4m3":
        vals = np.ascontiguousarray(words).view(ml_dtypes.float8_e4m3fn).astype(np.float64)
    else:
        nib = np.empty((g, p, n, 4), np.uint8)
        nib[..., 0::2] = words & 0xF
        nib[..., 1::2] = words >> 4
        vals = E2M1[nib]
    vals = vals * np.repeat(np.exp2(scales.astype(np.float64) - 127.0), 8, axis=1)[..., None]
    return vals.transpose(0, 1, 3, 2).reshape(g * 512, n)
def pack4(w):
    words, scales = pack_weight(w, "e2m1")
    return words.reshape(words.shape[0], 128, -1), scales


def unpack4(words, scales):
    return unpack_weight(words.reshape(words.shape[0], 128, -1, 2), scales, "e2m1")


E4M3FN = np.array([(-1.0 if i & 128 else 1.0) * ((1.0 + (i & 7) / 8.0) * 2.0 ** (((i >> 3) & 15) - 7) if i & 120 else (i & 7) * 2.0 ** -9) for i in range(256)])


def e4m3fn_bytes(y):
    return np.clip(np.asarray(y, np.float64), -448.0, 448.0).astype(np.float32).astype(ml_dtypes.float8_e4m3fn).view(np.uint8)


def e4m3fn_values(b):
    return E4M3FN[b]


J, L, N, D = 128, 16, 512, 1024


def draw0():
    a, t = mx_kscale(N), mx_kscale(D)
    level = np.random.uniform(0.5, 2.0, (J, 1, 1))
    s = bf(np.random.standard_normal((J, L, N)) * level * a)
    ydec_words, ydec_scales = pack4(np.random.standard_normal((N, D)) / np.sqrt(N) / a[:, None])
    thr = bf(np.random.uniform(0.2, 2.0, D))
    w = bf((1.0 + 0.1 * np.random.standard_normal(D)) * t)
    yenc_words, yenc_scales = pack4(np.random.standard_normal((D, N)) / np.sqrt(D) / t[:, None])
    return {"s": s,
            "ydec_words": ydec_words,
            "ydec_scales": ydec_scales,
            "thr": thr,
            "w": w,
            "yenc_words": yenc_words,
            "yenc_scales": yenc_scales}


def block_energy(d):
    return np.mean(np.square(d), axis=1)


def compressor_gain(e, thr):
    return np.power(1.0 + e / thr[None, :], -0.35)


def core(s, ydec_words, ydec_scales, thr, w, yenc_words, yenc_scales):
    d = mxq(f64(s), 2, "e4m3") @ unpack4(ydec_words, ydec_scales)
    e = block_energy(d)
    q = compressor_gain(e, f64(thr))
    c = d * q[:, None, :] * f64(w)[None, None, :]
    return mxq(c, 2, "e4m3") @ unpack4(yenc_words, yenc_scales)


def setup_inputs():
    drawn = draw0()
    full = np.asarray(drawn['s']).astype(np.float64)
    scale = (np.abs(full).reshape(128, 16, 4, 128).max(axis=(3,)) / 448.0).astype(np.float32)
    given = {}
    for key, value in drawn.items():
        if key == 's':
            given['s_bytes'] = e4m3fn_bytes(full / np.repeat(scale.astype(np.float64), 128, axis=2))
            given['s_scale'] = scale
        else:
            given[key] = value
    return given


def reference(s_bytes, s_scale, ydec_words, ydec_scales, thr, w, yenc_words, yenc_scales):
    return core(e4m3fn_values(s_bytes) * np.repeat(s_scale.astype(np.float64), 128, axis=2), ydec_words, ydec_scales, thr, w, yenc_words, yenc_scales)

from contextlib import ExitStack

import concourse.mybir as mybir
from concourse.masks import make_identity

F32 = mybir.dt.float32
BF16 = mybir.dt.bfloat16
U32 = mybir.dt.uint32
I32 = mybir.dt.int32
U8 = mybir.dt.uint8
FP8 = mybir.dt.float8_e4m3fn
FP8X4 = mybir.dt.float8_e4m3fn_x4
FP4X4 = mybir.dt.float4_e2m1fn_x4
ALU = mybir.AluOpType
ACT = mybir.ActivationFunctionType
AX = mybir.AxisListType

J, L, N, D = 128, 16, 512, 1024
FLOPS = 2 * 2 * J * L * N * D

P = 128
NQ = 4
BATCHES = ((0, 1), (2,), (3,))
PE_E = {(2, 1), (3, 1)}
LAG = 6
RATE = 2
A_V = (3, 3, 3, 0)
PSB = (2, 3, 2, 1)
BV = ()
HV = ()


def tile_ambisonicdirectionaldynamicrangecompress_d1p_kernel(
    tc, s_bytes, s_scale, ydec_words, ydec_scales, thr, w, yenc_words, yenc_scales, out
):
    nc = tc.nc
    with ExitStack() as ctx:
        keep = ctx.enter_context(tc.tile_pool(name="keep", bufs=1))
        work = ctx.enter_context(tc.tile_pool(name="work", bufs=2))
        psum = ctx.enter_context(tc.psum_pool(name="psum", bufs=1))

        s_raw = keep.tile([P, NQ, 4, N], U8, align_bytes=64)
        s_sc = keep.tile([P, NQ, 16], F32, align_bytes=64)
        yd_raw = keep.tile([P, 2 * D], U8, align_bytes=64)
        yd_sraw = keep.tile([P, D], U8, align_bytes=64)
        yd = keep.tile([P, 8, 256], U8, align_bytes=64)
        yd_sc = keep.tile([P, 8, P], U8, align_bytes=64)
        ye = keep.tile([P, 2, 2 * N], U8, align_bytes=64)
        ye_sc = keep.tile([P, 2, N], U8, align_bytes=64)
        thr_t = keep.tile([P, 2, 4], BF16, align_bytes=64)
        w_t = keep.tile([P, 2, 4], BF16, align_bytes=64)
        thr16 = keep.tile([P, 8], F32, align_bytes=64)
        rthr = keep.tile([P, 8], F32, align_bytes=64)
        ident = keep.tile([P, P], F32, align_bytes=64)
        warm = keep.tile([P, 1], F32, align_bytes=64)
        s_codes = keep.tile([P, NQ, 512], U32, align_bytes=64)
        s_csc = keep.tile([P, NQ, 512], U8, align_bytes=64)

        nc.vector.memset(yd_sraw[:].bitcast(U32), 0)
        nc.vector.memset(ye_sc[:].rearrange("p g n -> p (g n)").bitcast(U32), 0)

        s_rows = s_bytes.rearrange("j l k -> (j l) k").rearrange("(b p r) k -> b p r k", p=P, r=4)
        nc.sync.dma_start(out=s_sc[:], in_=s_scale.rearrange("j l q -> (j l) q").rearrange("(b p r) q -> p b (r q)", p=P, r=4))
        nc.sync.dma_start(out=s_raw[:, 0, 0:2, :], in_=s_rows[0][:, 0:2, :])
        nc.sync.dma_start(out=s_raw[:, 0, 2:4, :], in_=s_rows[0][:, 2:4, :])
        nc.sync.dma_start(out=yd_raw[:].bitcast(I32), in_=ydec_words[0].bitcast(I32))
        for Q in range(4):
            nc.scalar.dma_start(
                out=yd_sraw[32 * Q : 32 * Q + 4, :].bitcast(I32), in_=ydec_scales[0][4 * Q : 4 * Q + 4, :].bitcast(I32)
            )
        nc.vector.memset(warm[:], 1.0)
        nc.scalar.activation(out=warm[:], in_=warm[:], func=ACT.Ln)
        make_identity(nc, ident[:])
        nc.sync.dma_start(out=s_raw[:, 1, :, :], in_=s_rows[1])
        nc.sync.dma_start(out=thr_t[:], in_=thr.rearrange("(g p t) -> p g t", p=P, t=4))
        nc.sync.dma_start(out=w_t[:], in_=w.rearrange("(g p t) -> p g t", p=P, t=4))
        nc.sync.dma_start(out=s_raw[:, 2, :, :], in_=s_rows[2])
        nc.sync.dma_start(out=s_raw[:, 3, :, :], in_=s_rows[3])
        nc.sync.dma_start(
            out=ye[:].rearrange("p g n -> p g n").bitcast(I32), in_=yenc_words.rearrange("g p n -> p g n").bitcast(I32)
        )
        for Q in range(4):
            nc.sync.dma_start(
                out=ye_sc[32 * Q : 32 * Q + 4, :, :].bitcast(I32),
                in_=yenc_scales[:, 4 * Q : 4 * Q + 4, :].rearrange("g q n -> q g n").bitcast(I32),
            )

        sb = {}
        gq = {}
        xts = {}
        d_bank, d_sq, e_t = {}, {}, {}
        y_t, qw = {}, {}
        f_bank, cb, cc, ccs = {}, {}, {}, {}
        o_bank, o_sb = {}, {}

        def A(b, r, q, on_scalar):
            if (b,) not in sb:
                sb[(b,)] = work.tile([P, 4, N], BF16, align_bytes=64, tag="sb", name="sb")
            dst = sb[(b,)][:, r, 128 * q : 128 * q + 128]
            src = s_raw[:, b, r, 128 * q : 128 * q + 128].bitcast(FP8)
            sc = s_sc[:, b, 4 * r + q : 4 * r + q + 1]
            if on_scalar:
                nc.scalar.activation(out=dst, in_=src, func=ACT.Copy, scale=sc)
            else:
                nc.vector.tensor_scalar(out=dst, in0=src, scalar1=sc, scalar2=None, op0=ALU.mult)

        def T(b, h, tag):
            xt = psum.tile([P, 2, 2, P], F32, tag=tag, bufs=PS[tag], name="xt")
            xts[(b, h)] = xt
            for i in range(2):
                words = sb[(b,)][:, 2 * h + i, :].bitcast(F32)
                for u in range(2):
                    nc.tensor.transpose(xt[:, i, u, :], words[:, u : 2 * P : 2], ident[:])

        def B(b, h, on_scalar):
            if b not in gq:
                gq[b] = work.tile([P, 4, P, 4], BF16, align_bytes=64, tag="gq", name="gq")
            dst = gq[b][:, 2 * h : 2 * h + 2, :, :].rearrange("p r k t -> p (r k t)").bitcast(F32).rearrange(
                "p (r k u) -> p r k u", r=2, u=2
            )
            src = xts[(b, h)][:].rearrange("p r u k -> p r k u")
            if on_scalar:
                nc.scalar.copy(out=dst, in_=src)
            else:
                nc.vector.tensor_copy(out=dst, in_=src)

        def C(b):
            nc.vector.quantize_mx(
                out=s_codes[:, b, :].bitcast(FP8X4),
                scales=s_csc[:, b, :],
                in_=gq[b][:].rearrange("p r k t -> p (r k t)"),
            )

        def MM1(b, dt):
            bank = psum.tile([P, 512], F32, tag="d", bufs=PS["d"], name="dbank")
            d_bank[(b, dt)] = bank
            nc.tensor.matmul_mx(
                out=bank[:],
                lhsT=yd[:, dt, :].bitcast(FP4X4),
                lhsT_scale=yd_sc[:, dt, :],
                rhs=s_codes[:, b, :].bitcast(FP8X4),
                rhs_scale=s_csc[:, b, :],
                start=True,
                stop=True,
            )

        def SQ(b, dt):
            g, t = divmod(dt, 4)
            bank = d_bank[(b, dt)][:]
            if (b, g) in PE_E:
                if t == 0:
                    d_sq[(b, g)] = work.tile([P, 16, 4, 32], F32, tag="dsqt", bufs=2, name="dsqt", align_bytes=64)
                nc.scalar.activation(
                    out=d_sq[(b, g)][:, :, t, :].rearrange("p (r a) j -> p r a j", a=4),
                    in_=bank.rearrange("p (r j a) -> p r a j", r=4, a=4),
                    func=ACT.Square,
                )
            else:
                if t % 2 == 0:
                    d_sq[(b, dt // 2)] = work.tile([P, 2, 512], F32, tag="dsq", bufs=4, name="dsq", align_bytes=64)
                nc.scalar.activation(
                    out=d_sq[(b, dt // 2)][:, t % 2, :].rearrange("p (j r a) -> p j r a", r=4, a=4),
                    in_=bank.rearrange("p (r j a) -> p j r a", r=4, a=4),
                    func=ACT.Square,
                )

        def E(b, dt):
            g, t = divmod(dt, 4)
            if (b, g) in PE_E:
                if t == 3:
                    xt = psum.tile([P, 2, P], F32, tag="x", bufs=PS["x"], name="et")
                    for l in range(16):
                        nc.tensor.matmul(
                            xt[:, 0, :],
                            lhsT=d_sq[(b, g)][:, l, :, :].rearrange("p t j -> p (t j)"),
                            rhs=ident[:],
                            is_transpose=True,
                            start=(l == 0),
                            stop=(l == 15),
                        )
                    es = work.tile([P, P], F32, tag="es", bufs=2, name="es", align_bytes=64)
                    nc.scalar.copy(out=es[:], in_=xt[:, 0, :])
                    nc.tensor.transpose(xt[:, 1, :], es[:], ident[:])
                    e_t[(b, g)] = xt[:, 1, :].rearrange("p (t j) -> p t j", t=4)
                return
            if t % 2 == 0:
                return
            if (b, g) not in e_t:
                e_t[(b, g)] = work.tile([P, 4, 32], F32, tag="e", bufs=4, name="e", align_bytes=64)
            nc.vector.tensor_reduce(
                out=e_t[(b, g)][:, t - 1 : t + 1, :],
                in_=d_sq[(b, dt // 2)][:].rearrange("p d (j l) -> p d j l", l=16),
                axis=AX.X,
                op=ALU.add,
            )

        def Y(k, i, b, g):
            if k not in y_t:
                y_t[k] = work.tile([P, len(BATCHES[k]), 8, 32], F32, tag="y", bufs=2, name="y", align_bytes=64)
            src = e_t[(b, g)]
            nc.vector.tensor_tensor(
                out=y_t[k][:, i, 4 * g : 4 * g + 4, :],
                in0=src if (b, g) in PE_E else src[:],
                in1=rthr[:, 4 * g : 4 * g + 4].unsqueeze(2).to_broadcast([P, 4, 32]),
                op=ALU.mult,
            )

        def LNEXP(k):
            t = y_t[k][:].rearrange("p i d j -> p (i d j)")
            nc.scalar.activation(out=t, in_=t, func=ACT.Ln, bias=1.0)
            nc.scalar.activation(out=t, in_=t, func=ACT.Exp, scale=-0.35)

        def W(k, i, b):
            qw[b] = work.tile([P, 2, 32, 4], F32, tag="qw", bufs=4, name="qw", align_bytes=64)
            nc.vector.tensor_tensor(
                out=qw[b][:],
                in0=y_t[k][:, i, :, :].rearrange("p (g t) j -> p g j t", t=4),
                in1=w_t[:].unsqueeze(2).to_broadcast([P, 2, 32, 4]),
                op=ALU.mult,
            )

        def MM2(b, r, g):
            bank = psum.tile([P, 4, P], F32, tag="f", bufs=PS["f"], name="fbank")
            f_bank[(b, r, g)] = bank
            for t in range(4):
                nc.tensor.matmul_mx(
                    out=bank[:, t, :],
                    lhsT=yd[:, 4 * g + t, :].bitcast(FP4X4),
                    lhsT_scale=yd_sc[:, 4 * g + t, :],
                    rhs=s_codes[:, b, P * r : P * r + P].bitcast(FP8X4),
                    rhs_scale=s_csc[:, b, P * r : P * r + P],
                    start=True,
                    stop=True,
                )

        def F(b, r, g):
            if (b, r) not in cb:
                cb[(b, r)] = work.tile([P, 2, 32, 4, 4], BF16, tag="cb", bufs=3, name="cb", align_bytes=64)
            nc.vector.tensor_tensor(
                out=cb[(b, r)][:, g],
                in0=f_bank[(b, r, g)][:].rearrange("p t (j a) -> p j a t", a=4),
                in1=qw[b][:, g].unsqueeze(2).to_broadcast([P, 32, 4, 4]),
                op=ALU.mult,
            )

        def G(b, r):
            cc[(b, r)] = work.tile([P, 2, P], U32, tag="cc", bufs=3, name="cc", align_bytes=64)
            ccs[(b, r)] = work.tile([P, 2, P], U8, tag="ccs", bufs=3, name="ccs", align_bytes=64)
            nc.vector.quantize_mx(
                out=cc[(b, r)][:].rearrange("p g k -> p (g k)").bitcast(FP8X4),
                scales=ccs[(b, r)][:].rearrange("p g k -> p (g k)"),
                in_=cb[(b, r)][:].rearrange("p g j a t -> p (g j a t)"),
            )

        def ST2(b, r):
            bank = psum.tile([P, N], F32, tag="o", bufs=PS["o"], name="obank")
            o_bank[(b, r)] = bank
            for g in range(2):
                nc.tensor.matmul_mx(
                    out=bank[:],
                    lhsT=cc[(b, r)][:, g, :].bitcast(FP8X4),
                    lhsT_scale=ccs[(b, r)][:, g, :],
                    rhs=ye[:, g, :].bitcast(FP4X4),
                    rhs_scale=ye_sc[:, g, :],
                    start=(g == 0),
                    stop=(g == 1),
                )

        out_rows = out.rearrange("j l n -> (j l) n").rearrange("(b p r) n -> b p r n", p=P, r=4)

        def H(b, r, on_scalar=True):
            o = work.tile([P, N], F32, tag="osb", bufs=4, name="osb", align_bytes=64)
            if on_scalar:
                nc.scalar.copy(out=o[:], in_=o_bank[(b, r)][:])
            else:
                nc.vector.tensor_copy(out=o[:], in_=o_bank[(b, r)][:])
            nc.sync.dma_start(out=out_rows[b][:, r, :], in_=o[:])

        PS = {"d": PSB[0], "f": PSB[1], "o": PSB[2], "x": PSB[3]}

        for r in range(4):
            for q in range(4):
                A(0, r, q, q >= A_V[0])
        T(0, 0, "f")
        T(0, 1, "f")
        B(0, 0, True)
        B(0, 1, True)
        for g, eng in ((0, nc.vector), (1, nc.gpsimd)):
            eng.tensor_copy(
                out=yd[:, 4 * g : 4 * g + 4, :].rearrange("p t (m c) -> p t m c", c=2),
                in_=yd_raw[:, D * g : D * g + D].rearrange("p (m t c) -> p t m c", t=4, c=2),
            )
        nc.vector.tensor_copy(
            out=yd_sc[:].rearrange("p (g t) m -> p g t m", t=4),
            in_=yd_sraw[:].rearrange("p (g m t) -> p g t m", g=2, t=4),
        )
        C(0)
        nc.vector.tensor_scalar(
            out=thr16[:], in0=thr_t[:].rearrange("p g t -> p (g t)"), scalar1=16.0, scalar2=None, op0=ALU.mult
        )
        nc.vector.reciprocal(out=rthr[:], in_=thr16[:])

        def p2(b, r):
            for g in range(2):
                MM2(b, r, g)
                F(b, r, g)
            G(b, r)

        batch_of = {b: k for k, bs in enumerate(BATCHES) for b in bs}
        p2_list = [(b, r) for b in range(NQ) for r in range(4)]
        at = []
        pos = 0.0
        for b, r in p2_list:
            ready = 8 * (max(BATCHES[batch_of[b]]) + 1) + LAG
            pos = max(pos + RATE, ready)
            at.append(pos)
        state = {"last": None, "m": 0}

        def flush(slot):
            while state["m"] < 16 and at[state["m"]] <= slot:
                b, r = p2_list[state["m"]]
                if b not in qw:
                    W(batch_of[b], BATCHES[batch_of[b]].index(b), b)
                p2(b, r)
                if state["last"] is not None:
                    ST2(*state["last"])
                    H(*state["last"], on_scalar=state["last"] not in HV)
                state["last"] = (b, r)
                state["m"] += 1

        for b in range(NQ):
            nxt = b + 1 if b + 1 < NQ else None
            for dt in range(8):
                MM1(b, dt)
                SQ(b, dt)
                if nxt is not None:
                    if dt < 4:
                        for q in range(4):
                            A(nxt, dt, q, q >= A_V[nxt])
                    if dt == 3:
                        T(nxt, 0, "x")
                    if dt == 4:
                        B(nxt, 0, (nxt, 0) not in BV)
                    if dt == 5:
                        T(nxt, 1, "x")
                    if dt == 6:
                        B(nxt, 1, (nxt, 1) not in BV)
                E(b, dt)
                if dt in (3, 7):
                    Y(batch_of[b], BATCHES[batch_of[b]].index(b), b, dt // 4)
                flush(8 * b + dt)
            if nxt is not None:
                C(nxt)
            if b == max(BATCHES[batch_of[b]]):
                LNEXP(batch_of[b])
        flush(1000)
        ST2(*state["last"])
        H(*state["last"])
